import numpy as np
import ml_dtypes


def mxq(x, axis, fmt="e4m3"):
    dtype, down = {"e4m3": (ml_dtypes.float8_e4m3fn, 7), "e5m2": (ml_dtypes.float8_e5m2, 14)}[fmt]
    v = np.moveaxis(np.asarray(x, np.float32).astype(ml_dtypes.bfloat16).astype(np.float64), axis, -1)
    blocks = v.reshape(v.shape[:-1] + (-1, 32))
    amax = np.abs(blocks).max(-1, keepdims=True)
    byte = np.maximum(np.where(amax > 0, np.frexp(amax)[1] - 1 + 127, 0) - down, 1)
    scale = np.exp2(byte - 127.0)
    codes = (blocks / scale).astype(np.float32).astype(dtype).astype(np.float64)
    return np.moveaxis((codes * scale).reshape(v.shape), -1, axis)


WIDE = False


def mx_kscale(k):
    if not WIDE:
        return np.ones(k)
    levels = np.array([10, -10, 5, -5, 0])
    if k % 512:
        return np.exp2(np.random.permutation(np.resize(levels, k // 32))).repeat(32)
    a = np.empty((k // 512, 16))
    for p in range(k // 512):
        a[p, :8] = np.random.permutation(np.resize(levels, 8))
        for g in range(8):
            far = levels[np.abs(levels - a[p, g]) >= 10]
            a[p, g + 8] = far[np.random.randint(len(far))]
    return np.exp2(a.ravel()).repeat(32)


def f64(x):
    return np.asarray(x).astype(np.float64)


def striped(idx):
    return np.tile(idx.reshape(-1, 16).T, (8, 1)).astype(np.uint16)


def unstriped(offs):
    return offs[:16].T.reshape(-1).astype(np.int64)


def striped8(idx):
    return np.concatenate([x.reshape(-1, 16).T for x in idx]).astype(np.uint16)


def runs(offs, k):
    lists = np.stack([offs[16 * r : 16 * r + 16].T.reshape(-1) for r in range(8)]).astype(np.int64)
    return lists[np.arange(k) % 512 // 64]


def pack_weight(w):
    k, n = w.shape
    w = f64(np.asarray(w, np.float32).astype(ml_dtypes.bfloat16)).reshape(k // 32, 32, n)
    amax = np.abs(w).max(1)
    byte = np.clip(np.where(amax > 0, np.frexp(amax)[1] - 1 + 127 - 7, 1), 1, 254)
    scaled = (w * np.exp2(127.0 - byte)[:, None, :]).reshape(k, n).astype(np.float32)
    words = np.ascontiguousarray(scaled.reshape(k // 512, 128, 4, n).transpose(0, 1, 3, 2)).astype(ml_dtypes.float8_e4m3fn).view(np.uint8)
    return words, np.ascontiguousarray(byte.astype(np.uint8).reshape(k // 512, 16, n))


def unpack_weight(words, scales):
    g, p, n, _ = words.shape
    vals = np.ascontiguousarray(words).view(ml_dtypes.float8_e4m3fn).astype(np.float64) * np.repeat(np.exp2(scales.astype(np.float64) - 127.0), 8, axis=1)[..., None]
    return vals.transpose(0, 1, 3, 2).reshape(g * 512, n)


K, T, S, N, H = 512, 2048, 512, 512, 512


def setup_inputs():
    n = np.random.standard_normal
    s = mx_kscale(K)[:, None]
    u = mx_kscale(H)
    packed_xT = pack_weight(n((K, T)) * s)
    return {
        "x_words": packed_xT[0],
        "x_scales": packed_xT[1],
        "w1": (n((K, H)) / np.sqrt(K) / s).astype(np.float32),
        "gn": (np.random.uniform(0.5, 1.5, (H, 1)) * u[:, None]).astype(np.float32),
        "w2": (n((H, N)) / np.sqrt(H) / u[:, None]).astype(np.float32),
        "offs": striped(np.random.permutation(T)[:S]),
        "n1": striped(np.random.permutation(S)),
        "n2": striped(np.random.permutation(S)),
        "n3": striped8(np.stack([np.random.permutation(S) for _ in range(8)])),
        "n4": striped8(np.stack([np.random.permutation(S) for _ in range(8)])),
    }


def reference(x_words, x_scales, w1, gn, w2, offs, n1, n2, n3, n4):
    xq = unpack_weight(x_words, x_scales)[:, unstriped(offs)]
    y = mxq(f64(w1), 0, "e4m3").T @ xq
    z = f64(gn) * (y[:, unstriped(n1)] + 0.75 * y[:, unstriped(n2)])
    h = mxq(f64(w2), 0, "e4m3").T @ mxq(z, 0, "e4m3")
    return 0.75 * (h * (y[np.arange(H)[:, None], runs(n4, H)]) - ((h[np.arange(N)[:, None], runs(n3, N)]) * y))

@@ -1,0 +1,164 @@
+from contextlib import ExitStack
+
+import concourse.mybir as mybir
+
+K, T, S, H, N = 512, 2048, 512, 512, 512
+FLOPS = 2 * K * H * S + 2 * H * N * S
+
+F32 = mybir.dt.float32
+BF16 = mybir.dt.bfloat16
+I32 = mybir.dt.int32
+U32 = mybir.dt.uint32
+U16 = mybir.dt.uint16
+U8 = mybir.dt.uint8
+FP8X4 = mybir.dt.float8_e4m3fn_x4
+COPY = mybir.ActivationFunctionType.Copy
+MULT = mybir.AluOpType.mult
+ADD = mybir.AluOpType.add
+SUB = mybir.AluOpType.subtract
+
+P = 128
+PACK = 4
+HALF = S // 2
+
+
+def entries(lst, start, count):
+    return lst[:, start // 16 : (start + count) // 16]
+
+
+def tile_picked_skipcrossbsum_none_p_kernel(tc, x_words, x_scales, w1, gn, w2, offs, n1, n2, n3, n4, out):
+    nc = tc.nc
+    with ExitStack() as ctx:
+        keep = ctx.enter_context(tc.tile_pool(name="keep", bufs=1))
+        psum = ctx.enter_context(tc.psum_pool(name="psum", bufs=1))
+
+        def sb(name, shape, dtype, tag=None):
+            return keep.tile(shape, dtype, name=name, tag=tag or name, align_bytes=64)
+
+        lists = {name: keep.tile([P, S // 16], U16, name="list_" + name) for name in ("offs", "n1", "n2", "n3", "n4")}
+        x_w = sb("x_w", [P, T], U32)
+        x_s = sb("x_s", [P, T], U8)
+        w1_raw = sb("w1_raw", [P, PACK, H], F32)
+        w2_raw = sb("w2_raw", [P, PACK, N], F32)
+        gain = sb("gain", [P, PACK], F32)
+
+        nc.vector.memset(x_s[:].bitcast(I32), 0)
+        nc.sync.dma_start(lists["offs"][:], offs)
+        nc.sync.dma_start(w1_raw[:], w1.rearrange("(p j) c -> p j c", j=PACK))
+        nc.sync.dma_start(x_w[:].bitcast(I32), x_words[0].rearrange("p n r -> p (n r)").bitcast(I32))
+        for q in range(4):
+            nc.scalar.dma_start(x_s[32 * q : 32 * q + 4, :].bitcast(I32), x_scales[0, 4 * q : 4 * q + 4, :].bitcast(I32))
+        nc.sync.dma_start(gain[:], gn.rearrange("(p t) o -> p (t o)", t=PACK))
+        nc.sync.dma_start(lists["n1"][:], n1)
+        nc.sync.dma_start(lists["n2"][:], n2)
+        nc.sync.dma_start(w2_raw[:], w2.rearrange("(p j) c -> p j c", j=PACK))
+        nc.sync.dma_start(lists["n4"][:], n4)
+        nc.sync.dma_start(lists["n3"][:], n3)
+
+        xq_s = sb("xq_s", [P, S], U8)
+        nc.vector.tensor_copy(xq_s[:], x_s[:].indirect(lists["offs"][:]))
+
+        def dealt(raw, u):
+            return raw[:].rearrange("p j (m t) -> p t m j", t=PACK)[:, 2 * u : 2 * u + 2]
+
+        def quantised(name, src, words):
+            codes = sb(name + "_codes", [P, words], U32)
+            scales = sb(name + "_scales", [P, words], U8)
+            nc.vector.quantize_mx(out=codes[:].bitcast(FP8X4), scales=scales[:], in_=src)
+            return codes, scales
+
+        w1_bf = [sb("w1_bf%d" % u, [P, 2, P, PACK], BF16) for u in range(2)]
+        nc.vector.tensor_copy(w1_bf[0][:], dealt(w1_raw, 0))
+        nc.scalar.activation(w1_bf[1][:], dealt(w1_raw, 1), COPY)
+        w1_q = [quantised("w1q%d" % u, w1_bf[u][:].rearrange("p t m j -> p (t m j)"), 2 * P) for u in range(2)]
+
+        xq_w = sb("xq_w", [P, S], U32)
+        for c in range(2):
+            nc.vector.tensor_copy(xq_w[:, c * HALF : (c + 1) * HALF], x_w[:].indirect(entries(lists["offs"], c * HALF, HALF)))
+
+        def product(bank, w_q, t, codes, scales):
+            w_codes, w_scales = w_q[t // 2]
+            cols = slice((t % 2) * P, (t % 2 + 1) * P)
+            nc.tensor.matmul_mx(out=bank, lhsT=w_codes[:, cols].bitcast(FP8X4), lhsT_scale=w_scales[:, cols],
+                                rhs=codes.bitcast(FP8X4), rhs_scale=scales, start=True, stop=True)
+
+        halves = [slice(0, HALF), slice(HALF, S)]
+        gy = [sb("gy%d" % t, [P, S], F32) for t in range(PACK)]
+        y0 = [psum.tile([P, HALF], F32, name="y0_%d" % c, tag="bank%d" % c) for c in range(2)]
+        for c in range(2):
+            product(y0[c][:], w1_q, 0, xq_w[:, halves[c]], xq_s[:, halves[c]])
+            nc.scalar.activation(gy[0][:, halves[c]], y0[c][:], COPY, scale=gain[:, 0:1])
+        y = [None] + [psum.tile([P, S], F32, name="y%d" % t, tag="bank%d" % (t + 1)) for t in range(1, PACK)]
+        for t in range(1, PACK):
+            product(y[t][:], w1_q, t, xq_w[:], xq_s[:])
+            nc.vector.tensor_scalar(gy[t][:], y[t][:], gain[:, t : t + 1], None, MULT)
+
+        w2_bf = sb("w2_bf", [P, PACK, P, PACK], BF16)
+        nc.vector.tensor_copy(w2_bf[:], w2_raw[:].rearrange("p j (m t) -> p t m j", t=PACK))
+        w2_codes, w2_scales = quantised("w2q", w2_bf[:].rearrange("p t m j -> p (t m j)"), PACK * P)
+        w2_q = [(w2_codes[:, u * 2 * P : (u + 1) * 2 * P], w2_scales[:, u * 2 * P : (u + 1) * 2 * P]) for u in range(2)]
+
+        h_bank = [psum.tile([P, S], F32, name="h%d" % t, tag="bank%d" % ((t + 5) % 8)) for t in range(PACK)]
+        h = [sb("hs%d" % t, [P, S], F32) for t in range(PACK)]
+
+        def z_half(c, g1, g2):
+            for t in range(PACK):
+                nc.scalar.activation(g1[:, t, :], gy[t][:].indirect(entries(lists["n1"], c * HALF, HALF)), COPY)
+                nc.scalar.activation(g2[:, t, :], gy[t][:].indirect(entries(lists["n2"], c * HALF, HALF)), COPY, scale=0.75)
+            z_bf = sb("z_bf%d" % c, [P, HALF, PACK], BF16, tag=("w2_raw", "zq0_codes")[c])
+            nc.vector.tensor_tensor(z_bf[:].rearrange("p (c i) t -> p c t i", i=4),
+                                    g1.rearrange("p t (c i) -> p c t i", i=4),
+                                    g2.rearrange("p t (c i) -> p c t i", i=4), ADD)
+            return quantised("zq%d" % c, z_bf[:].rearrange("p s t -> p (s t)"), HALF)
+
+        def h_half(c, t, z_q):
+            product(h_bank[t][:, halves[c]], w2_q, t, z_q[0][:], z_q[1][:])
+            nc.vector.tensor_copy(h[t][:, halves[c]], h_bank[t][:, halves[c]])
+
+        ys = [sb("ys%d" % t, [P, S], F32) for t in range(PACK)]
+        for c in range(2):
+            nc.vector.tensor_scalar(ys[0][:, halves[c]], y0[c][:], 0.75, None, MULT)
+        z_q = z_half(0, sb("g1_0", [P, PACK, HALF], F32)[:], sb("g2_0", [P, PACK, HALF], F32)[:])
+        for t in range(PACK):
+            h_half(0, t, z_q)
+        for t in range(1, PACK):
+            nc.vector.tensor_scalar(ys[t][:], y[t][:], 0.75, None, MULT)
+        g_late = sb("g_late", [P, 2, PACK, HALF], F32, tag="gain")
+        z_q = z_half(1, g_late[:, 0], g_late[:, 1])
+
+        out_rows = out.rearrange("(p t) s -> p t s", t=PACK)
+        first = [sb("first%d" % t, [P, S], F32) for t in range(PACK)]
+
+        def fetch_y(t):
+            y4 = sb("y4_%d" % t, [P, S], F32, tag=("g1_0", "g2_0")[t % 2])
+            for c in range(2):
+                nc.scalar.activation(y4[:, halves[c]], ys[t][:].indirect(entries(lists["n4"], c * HALF, HALF)), COPY)
+            nc.vector.tensor_tensor(first[t][:], h_bank[t][:], y4[:], MULT)
+
+        def finish(t, pieces):
+            h3 = sb("h3_%d" % t, [P, S], F32)
+            second = sb("second%d" % t, [P, S], F32)
+            res = sb("res%d" % t, [P, S], F32)
+            start = 0
+            for widths in pieces:
+                lo = start
+                for width in widths:
+                    nc.scalar.activation(h3[:, start : start + width], h[t][:].indirect(entries(lists["n3"], start, width)), COPY)
+                    start = start + width
+                cols = slice(lo, start)
+                nc.vector.tensor_tensor(second[:, cols], h3[:, cols], ys[t][:, cols], MULT)
+                nc.vector.tensor_tensor(res[:, cols], first[t][:, cols], second[:, cols], SUB)
+                nc.sync.dma_start(out_rows[:, t, cols], res[:, cols])
+
+        h_half(1, 0, z_q)
+        fetch_y(0)
+        h_half(1, 1, z_q)
+        fetch_y(1)
+        finish(0, [[HALF, HALF]])
+        h_half(1, 2, z_q)
+        h_half(1, 3, z_q)
+        fetch_y(2)
+        finish(1, [[HALF, HALF]])
+        fetch_y(3)
+        finish(2, [[HALF, HALF]])
+        finish(3, [[HALF], [128], [128]])

@@ -43,11 +43,11 @@ def tile_picked_skipcrossbsum_none_p_kernel(tc, x_words, x_scales, w1, gn, w2, o
         gain = sb("gain", [P, PACK], F32)
 
         nc.vector.memset(x_s[:].bitcast(I32), 0)
-        nc.sync.dma_start(lists["offs"][:], offs)
         nc.sync.dma_start(w1_raw[:], w1.rearrange("(p j) c -> p j c", j=PACK))
-        nc.sync.dma_start(x_w[:].bitcast(I32), x_words[0].rearrange("p n r -> p (n r)").bitcast(I32))
+        nc.sync.dma_start(lists["offs"][:], offs)
         for q in range(4):
-            nc.scalar.dma_start(x_s[32 * q : 32 * q + 4, :].bitcast(I32), x_scales[0, 4 * q : 4 * q + 4, :].bitcast(I32))
+            nc.sync.dma_start(x_s[32 * q : 32 * q + 4, :].bitcast(I32), x_scales[0, 4 * q : 4 * q + 4, :].bitcast(I32))
+        nc.sync.dma_start(x_w[:].bitcast(I32), x_words[0].rearrange("p n r -> p (n r)").bitcast(I32))
         nc.sync.dma_start(gain[:], gn.rearrange("(p t) o -> p (t o)", t=PACK))
         nc.sync.dma_start(lists["n1"][:], n1)
         nc.sync.dma_start(lists["n2"][:], n2)
@@ -55,35 +55,39 @@ def tile_picked_skipcrossbsum_none_p_kernel(tc, x_words, x_scales, w1, gn, w2, o
         nc.sync.dma_start(lists["n4"][:], n4)
         nc.sync.dma_start(lists["n3"][:], n3)
 
-        xq_s = sb("xq_s", [P, S], U8)
-        nc.vector.tensor_copy(xq_s[:], x_s[:].indirect(lists["offs"][:]))
+        def dealing_views(raw, dealt):
+            return raw[:].rearrange("p j (m t) -> p m j t", t=PACK), dealt[:].rearrange("p t m j -> p m j t")
 
-        def dealt(raw, u):
-            return raw[:].rearrange("p j (m t) -> p t m j", t=PACK)[:, 2 * u : 2 * u + 2]
-
-        def quantised(name, src, words):
-            codes = sb(name + "_codes", [P, words], U32)
+        def quantised(name, src, words, tag=None):
+            codes = sb(name + "_codes", [P, words], U32, tag=tag)
             scales = sb(name + "_scales", [P, words], U8)
             nc.vector.quantize_mx(out=codes[:].bitcast(FP8X4), scales=scales[:], in_=src)
             return codes, scales
 
-        w1_bf = [sb("w1_bf%d" % u, [P, 2, P, PACK], BF16) for u in range(2)]
-        nc.vector.tensor_copy(w1_bf[0][:], dealt(w1_raw, 0))
-        nc.scalar.activation(w1_bf[1][:], dealt(w1_raw, 1), COPY)
-        w1_q = [quantised("w1q%d" % u, w1_bf[u][:].rearrange("p t m j -> p (t m j)"), 2 * P) for u in range(2)]
+        w1_bf = sb("w1_bf", [P, PACK, P, PACK], BF16)
+        src, dst = dealing_views(w1_raw, w1_bf)
+        nc.vector.tensor_copy(dst[:, : P // 2], src[:, : P // 2])
+        nc.scalar.activation(dst[:, P // 2 :], src[:, P // 2 :], COPY)
+        xq_s = sb("xq_s", [P, S], U8)
+        nc.vector.tensor_copy(xq_s[:], x_s[:].indirect(lists["offs"][:]))
+        w1_q = quantised("w1q", w1_bf[:].rearrange("p t m j -> p (t m j)"), PACK * P, tag="x_s")
 
         xq_w = sb("xq_w", [P, S], U32)
         for c in range(2):
             nc.vector.tensor_copy(xq_w[:, c * HALF : (c + 1) * HALF], x_w[:].indirect(entries(lists["offs"], c * HALF, HALF)))
 
         def product(bank, w_q, t, codes, scales):
-            w_codes, w_scales = w_q[t // 2]
-            cols = slice((t % 2) * P, (t % 2 + 1) * P)
+            w_codes, w_scales = w_q
+            cols = slice(t * P, (t + 1) * P)
             nc.tensor.matmul_mx(out=bank, lhsT=w_codes[:, cols].bitcast(FP8X4), lhsT_scale=w_scales[:, cols],
                                 rhs=codes.bitcast(FP8X4), rhs_scale=scales, start=True, stop=True)
 
         halves = [slice(0, HALF), slice(HALF, S)]
-        gy = [sb("gy%d" % t, [P, S], F32) for t in range(PACK)]
+        last = PACK - 1
+        y_win = [sb("y_win%d" % t, [P, 2 * S], F32) for t in range(last)]
+        h_last = sb("h_win_last", [P, 2 * S], F32)
+        ys = [y_win[t][:, :S] for t in range(last)]
+        gy = [y_win[t][:, S:] for t in range(last)] + [h_last[:, S:]]
         y0 = [psum.tile([P, HALF], F32, name="y0_%d" % c, tag="bank%d" % c) for c in range(2)]
         for c in range(2):
             product(y0[c][:], w1_q, 0, xq_w[:, halves[c]], xq_s[:, halves[c]])
@@ -91,74 +95,71 @@ def tile_picked_skipcrossbsum_none_p_kernel(tc, x_words, x_scales, w1, gn, w2, o
         y = [None] + [psum.tile([P, S], F32, name="y%d" % t, tag="bank%d" % (t + 1)) for t in range(1, PACK)]
         for t in range(1, PACK):
             product(y[t][:], w1_q, t, xq_w[:], xq_s[:])
-            nc.vector.tensor_scalar(gy[t][:], y[t][:], gain[:, t : t + 1], None, MULT)
+            nc.vector.tensor_scalar(gy[t], y[t][:], gain[:, t : t + 1], None, MULT)
 
         w2_bf = sb("w2_bf", [P, PACK, P, PACK], BF16)
-        nc.vector.tensor_copy(w2_bf[:], w2_raw[:].rearrange("p j (m t) -> p t m j", t=PACK))
-        w2_codes, w2_scales = quantised("w2q", w2_bf[:].rearrange("p t m j -> p (t m j)"), PACK * P)
-        w2_q = [(w2_codes[:, u * 2 * P : (u + 1) * 2 * P], w2_scales[:, u * 2 * P : (u + 1) * 2 * P]) for u in range(2)]
+        src, dst = dealing_views(w2_raw, w2_bf)
+        nc.vector.tensor_copy(dst, src)
+        w2_q = quantised("w2q", w2_bf[:].rearrange("p t m j -> p (t m j)"), PACK * P)
+        for c in range(2):
+            nc.vector.tensor_scalar(ys[0][:, halves[c]], y0[c][:], 0.75, None, MULT)
 
         h_bank = [psum.tile([P, S], F32, name="h%d" % t, tag="bank%d" % ((t + 5) % 8)) for t in range(PACK)]
-        h = [sb("hs%d" % t, [P, S], F32) for t in range(PACK)]
 
         def z_half(c, g1, g2):
             for t in range(PACK):
-                nc.scalar.activation(g1[:, t, :], gy[t][:].indirect(entries(lists["n1"], c * HALF, HALF)), COPY)
-                nc.scalar.activation(g2[:, t, :], gy[t][:].indirect(entries(lists["n2"], c * HALF, HALF)), COPY, scale=0.75)
+                nc.scalar.activation(g1[:, t, :], gy[t].indirect(entries(lists["n1"], c * HALF, HALF)), COPY)
+                nc.scalar.activation(g2[:, t, :], gy[t].indirect(entries(lists["n2"], c * HALF, HALF)), COPY, scale=0.75)
             z_bf = sb("z_bf%d" % c, [P, HALF, PACK], BF16, tag=("w2_raw", "zq0_codes")[c])
             nc.vector.tensor_tensor(z_bf[:].rearrange("p (c i) t -> p c t i", i=4),
                                     g1.rearrange("p t (c i) -> p c t i", i=4),
                                     g2.rearrange("p t (c i) -> p c t i", i=4), ADD)
             return quantised("zq%d" % c, z_bf[:].rearrange("p s t -> p (s t)"), HALF)
 
-        def h_half(c, t, z_q):
-            product(h_bank[t][:, halves[c]], w2_q, t, z_q[0][:], z_q[1][:])
-            nc.vector.tensor_copy(h[t][:, halves[c]], h_bank[t][:, halves[c]])
+        def h_half(c, z_q):
+            for t in range(PACK):
+                product(h_bank[t][:, halves[c]], w2_q, t, z_q[0][:], z_q[1][:])
+                nc.vector.tensor_copy(h_win[t][:, halves[c]], h_bank[t][:, halves[c]])
 
-        ys = [sb("ys%d" % t, [P, S], F32) for t in range(PACK)]
-        for c in range(2):
-            nc.vector.tensor_scalar(ys[0][:, halves[c]], y0[c][:], 0.75, None, MULT)
         z_q = z_half(0, sb("g1_0", [P, PACK, HALF], F32)[:], sb("g2_0", [P, PACK, HALF], F32)[:])
-        for t in range(PACK):
-            h_half(0, t, z_q)
-        for t in range(1, PACK):
-            nc.vector.tensor_scalar(ys[t][:], y[t][:], 0.75, None, MULT)
+        h_win = [sb("h_win%d" % t, [P, 2 * S], F32, tag=tag) for t, tag in enumerate(("g1_0", "g2_0", None))] + [h_last]
+        h_half(0, z_q)
+        for t in range(1, last):
+            nc.vector.tensor_scalar(ys[t], y[t][:], 0.75, None, MULT)
         g_late = sb("g_late", [P, 2, PACK, HALF], F32, tag="gain")
         z_q = z_half(1, g_late[:, 0], g_late[:, 1])
+        h_half(1, z_q)
+        y_win.append(sb("y_win_last", [P, S], F32, tag="zq0_codes"))
+        ys.append(y_win[last][:])
+        nc.vector.tensor_scalar(ys[last], y[last][:], 0.75, None, MULT)
 
         out_rows = out.rearrange("(p t) s -> p t s", t=PACK)
         first = [sb("first%d" % t, [P, S], F32) for t in range(PACK)]
+        second = [sb("second%d" % t, [P, S], F32) for t in range(PACK)]
+        res = [sb("res%d" % t, [P, S], F32) for t in range(PACK)]
 
-        def fetch_y(t):
-            y4 = sb("y4_%d" % t, [P, S], F32, tag=("g1_0", "g2_0")[t % 2])
-            for c in range(2):
-                nc.scalar.activation(y4[:, halves[c]], ys[t][:].indirect(entries(lists["n4"], c * HALF, HALF)), COPY)
-            nc.vector.tensor_tensor(first[t][:], h_bank[t][:], y4[:], MULT)
+        def first_term(t, fetched, start, width):
+            cols = slice(start, start + width)
+            nc.scalar.activation(fetched[:, cols], y_win[t][:].indirect(entries(lists["n4"], start, width)), COPY)
+            nc.vector.tensor_tensor(first[t][:, cols], h_bank[t][:, cols], fetched[:, cols], MULT)
 
-        def finish(t, pieces):
+        def second_term(t):
             h3 = sb("h3_%d" % t, [P, S], F32)
-            second = sb("second%d" % t, [P, S], F32)
-            res = sb("res%d" % t, [P, S], F32)
-            start = 0
-            for widths in pieces:
-                lo = start
-                for width in widths:
-                    nc.scalar.activation(h3[:, start : start + width], h[t][:].indirect(entries(lists["n3"], start, width)), COPY)
-                    start = start + width
-                cols = slice(lo, start)
-                nc.vector.tensor_tensor(second[:, cols], h3[:, cols], ys[t][:, cols], MULT)
-                nc.vector.tensor_tensor(res[:, cols], first[t][:, cols], second[:, cols], SUB)
-                nc.sync.dma_start(out_rows[:, t, cols], res[:, cols])
+            nc.scalar.activation(h3[:], h_win[t][:].indirect(lists["n3"][:]), COPY)
+            nc.vector.tensor_tensor(second[t][:], h3[:], ys[t], MULT)
 
-        h_half(1, 0, z_q)
-        fetch_y(0)
-        h_half(1, 1, z_q)
-        fetch_y(1)
-        finish(0, [[HALF, HALF]])
-        h_half(1, 2, z_q)
-        h_half(1, 3, z_q)
-        fetch_y(2)
-        finish(1, [[HALF, HALF]])
-        fetch_y(3)
-        finish(2, [[HALF, HALF]])
-        finish(3, [[HALF], [128], [128]])
+        def finish(t, start, width):
+            cols = slice(start, start + width)
+            nc.vector.tensor_tensor(res[t][:, cols], first[t][:, cols], second[t][:, cols], SUB)
+            nc.sync.dma_start(out_rows[:, t, cols], res[t][:, cols])
+
+        for t in range(last):
+            first_term(t, h_win[t][:, S:], 0, S)
+        for t in range(last):
+            second_term(t)
+            finish(t, 0, S)
+        second_term(last)
+        y4_last = sb("y4_last", [P, S], F32, tag="g1_0")
+        for start, width in ((0, HALF), (HALF, HALF // 2), (HALF + HALF // 2, HALF // 2)):
+            first_term(last, y4_last[:], start, width)
+            finish(last, start, width)

@@ -70,11 +70,13 @@ def tile_picked_skipcrossbsum_none_p_kernel(tc, x_words, x_scales, w1, gn, w2, o
         nc.scalar.activation(dst[:, P // 2 :], src[:, P // 2 :], COPY)
         xq_s = sb("xq_s", [P, S], U8)
         nc.vector.tensor_copy(xq_s[:], x_s[:].indirect(lists["offs"][:]))
-        w1_q = quantised("w1q", w1_bf[:].rearrange("p t m j -> p (t m j)"), PACK * P, tag="x_s")
+        w1_first = quantised("w1q_first", w1_bf[:, 0].rearrange("p m j -> p (m j)"), P, tag="x_s")
 
         xq_w = sb("xq_w", [P, S], U32)
         for c in range(2):
             nc.vector.tensor_copy(xq_w[:, c * HALF : (c + 1) * HALF], x_w[:].indirect(entries(lists["offs"], c * HALF, HALF)))
+
+        w1_rest = quantised("w1q_rest", w1_bf[:, 1:].rearrange("p t m j -> p (t m j)"), (PACK - 1) * P, tag="x_w")
 
         def product(bank, w_q, t, codes, scales):
             w_codes, w_scales = w_q
@@ -90,11 +92,11 @@ def tile_picked_skipcrossbsum_none_p_kernel(tc, x_words, x_scales, w1, gn, w2, o
         gy = [y_win[t][:, S:] for t in range(last)] + [h_last[:, S:]]
         y0 = [psum.tile([P, HALF], F32, name="y0_%d" % c, tag="bank%d" % c) for c in range(2)]
         for c in range(2):
-            product(y0[c][:], w1_q, 0, xq_w[:, halves[c]], xq_s[:, halves[c]])
+            product(y0[c][:], w1_first, 0, xq_w[:, halves[c]], xq_s[:, halves[c]])
             nc.scalar.activation(gy[0][:, halves[c]], y0[c][:], COPY, scale=gain[:, 0:1])
         y = [None] + [psum.tile([P, S], F32, name="y%d" % t, tag="bank%d" % (t + 1)) for t in range(1, PACK)]
         for t in range(1, PACK):
-            product(y[t][:], w1_q, t, xq_w[:], xq_s[:])
+            product(y[t][:], w1_rest, t - 1, xq_w[:], xq_s[:])
             nc.vector.tensor_scalar(gy[t], y[t][:], gain[:, t : t + 1], None, MULT)
 
         w2_bf = sb("w2_bf", [P, PACK, P, PACK], BF16)
@@ -148,18 +150,18 @@ def tile_picked_skipcrossbsum_none_p_kernel(tc, x_words, x_scales, w1, gn, w2, o
             nc.scalar.activation(h3[:], h_win[t][:].indirect(lists["n3"][:]), COPY)
             nc.vector.tensor_tensor(second[t][:], h3[:], ys[t], MULT)
 
-        def finish(t, start, width):
+        def finish(engine, t, start, width):
             cols = slice(start, start + width)
-            nc.vector.tensor_tensor(res[t][:, cols], first[t][:, cols], second[t][:, cols], SUB)
+            engine.tensor_tensor(res[t][:, cols], first[t][:, cols], second[t][:, cols], SUB)
             nc.sync.dma_start(out_rows[:, t, cols], res[t][:, cols])
 
         for t in range(last):
             first_term(t, h_win[t][:, S:], 0, S)
         for t in range(last):
             second_term(t)
-            finish(t, 0, S)
+            finish(nc.vector, t, 0, S)
         second_term(last)
         y4_last = sb("y4_last", [P, S], F32, tag="g1_0")
         for start, width in ((0, HALF), (HALF, HALF // 2), (HALF + HALF // 2, HALF // 2)):
             first_term(last, y4_last[:], start, width)
-            finish(last, start, width)
+            finish(nc.vector, last, start, width)

from contextlib import ExitStack

import concourse.mybir as mybir

K, T, S, H, N = 512, 2048, 512, 512, 512
FLOPS = 2 * K * H * S + 2 * H * N * S

F32 = mybir.dt.float32
BF16 = mybir.dt.bfloat16
I32 = mybir.dt.int32
U32 = mybir.dt.uint32
U16 = mybir.dt.uint16
U8 = mybir.dt.uint8
FP8X4 = mybir.dt.float8_e4m3fn_x4
COPY = mybir.ActivationFunctionType.Copy
MULT = mybir.AluOpType.mult
ADD = mybir.AluOpType.add
SUB = mybir.AluOpType.subtract

P = 128
PACK = 4
HALF = S // 2


def entries(lst, start, count):
    return lst[:, start // 16 : (start + count) // 16]


def tile_picked_skipcrossbsum_none_p_kernel(tc, x_words, x_scales, w1, gn, w2, offs, n1, n2, n3, n4, out):
    nc = tc.nc
    with ExitStack() as ctx:
        keep = ctx.enter_context(tc.tile_pool(name="keep", bufs=1))
        psum = ctx.enter_context(tc.psum_pool(name="psum", bufs=1))

        def sb(name, shape, dtype, tag=None):
            return keep.tile(shape, dtype, name=name, tag=tag or name, align_bytes=64)

        lists = {name: keep.tile([P, S // 16], U16, name="list_" + name) for name in ("offs", "n1", "n2", "n3", "n4")}
        x_w = sb("x_w", [P, T], U32)
        x_s = sb("x_s", [P, T], U8)
        w1_raw = sb("w1_raw", [P, PACK, H], F32)
        w2_raw = sb("w2_raw", [P, PACK, N], F32)
        gain = sb("gain", [P, PACK], F32)

        nc.vector.memset(x_s[:].bitcast(I32), 0)
        nc.sync.dma_start(w1_raw[:], w1.rearrange("(p j) c -> p j c", j=PACK))
        nc.sync.dma_start(lists["offs"][:], offs)
        for q in range(4):
            nc.sync.dma_start(x_s[32 * q : 32 * q + 4, :].bitcast(I32), x_scales[0, 4 * q : 4 * q + 4, :].bitcast(I32))
        nc.sync.dma_start(x_w[:].bitcast(I32), x_words[0].rearrange("p n r -> p (n r)").bitcast(I32))
        nc.sync.dma_start(gain[:], gn.rearrange("(p t) o -> p (t o)", t=PACK))
        nc.sync.dma_start(lists["n1"][:], n1)
        nc.sync.dma_start(lists["n2"][:], n2)
        nc.sync.dma_start(w2_raw[:], w2.rearrange("(p j) c -> p j c", j=PACK))
        nc.sync.dma_start(lists["n4"][:], n4)
        nc.sync.dma_start(lists["n3"][:], n3)

        def dealing_views(raw, dealt):
            return raw[:].rearrange("p j (m t) -> p m j t", t=PACK), dealt[:].rearrange("p t m j -> p m j t")

        def quantised(name, src, words, tag=None):
            codes = sb(name + "_codes", [P, words], U32, tag=tag)
            scales = sb(name + "_scales", [P, words], U8)
            nc.vector.quantize_mx(out=codes[:].bitcast(FP8X4), scales=scales[:], in_=src)
            return codes, scales

        w1_bf = sb("w1_bf", [P, PACK, P, PACK], BF16)
        src, dst = dealing_views(w1_raw, w1_bf)
        nc.vector.tensor_copy(dst[:, : P // 2], src[:, : P // 2])
        nc.scalar.activation(dst[:, P // 2 :], src[:, P // 2 :], COPY)
        xq_s = sb("xq_s", [P, S], U8)
        nc.vector.tensor_copy(xq_s[:], x_s[:].indirect(lists["offs"][:]))
        w1_first = quantised("w1q_first", w1_bf[:, 0].rearrange("p m j -> p (m j)"), P, tag="x_s")

        xq_w = sb("xq_w", [P, S], U32)
        for c in range(2):
            nc.vector.tensor_copy(xq_w[:, c * HALF : (c + 1) * HALF], x_w[:].indirect(entries(lists["offs"], c * HALF, HALF)))

        w1_rest = quantised("w1q_rest", w1_bf[:, 1:].rearrange("p t m j -> p (t m j)"), (PACK - 1) * P, tag="x_w")

        def product(bank, w_q, t, codes, scales):
            w_codes, w_scales = w_q
            cols = slice(t * P, (t + 1) * P)
            nc.tensor.matmul_mx(out=bank, lhsT=w_codes[:, cols].bitcast(FP8X4), lhsT_scale=w_scales[:, cols],
                                rhs=codes.bitcast(FP8X4), rhs_scale=scales, start=True, stop=True)

        halves = [slice(0, HALF), slice(HALF, S)]
        last = PACK - 1
        y_win = [sb("y_win%d" % t, [P, 2 * S], F32) for t in range(last)]
        h_last = sb("h_win_last", [P, 2 * S], F32)
        ys = [y_win[t][:, :S] for t in range(last)]
        gy = [y_win[t][:, S:] for t in range(last)] + [h_last[:, S:]]
        y0 = [psum.tile([P, HALF], F32, name="y0_%d" % c, tag="bank%d" % c) for c in range(2)]
        for c in range(2):
            product(y0[c][:], w1_first, 0, xq_w[:, halves[c]], xq_s[:, halves[c]])
            nc.scalar.activation(gy[0][:, halves[c]], y0[c][:], COPY, scale=gain[:, 0:1])
        y = [None] + [psum.tile([P, S], F32, name="y%d" % t, tag="bank%d" % (t + 1)) for t in range(1, PACK)]
        for t in range(1, PACK):
            product(y[t][:], w1_rest, t - 1, xq_w[:], xq_s[:])
            nc.vector.tensor_scalar(gy[t], y[t][:], gain[:, t : t + 1], None, MULT)

        w2_bf = sb("w2_bf", [P, PACK, P, PACK], BF16)
        src, dst = dealing_views(w2_raw, w2_bf)
        nc.vector.tensor_copy(dst, src)
        w2_q = quantised("w2q", w2_bf[:].rearrange("p t m j -> p (t m j)"), PACK * P)
        for c in range(2):
            nc.vector.tensor_scalar(ys[0][:, halves[c]], y0[c][:], 0.75, None, MULT)

        h_bank = [psum.tile([P, S], F32, name="h%d" % t, tag="bank%d" % ((t + 5) % 8)) for t in range(PACK)]

        def z_half(c, g1, g2):
            for t in range(PACK):
                nc.scalar.activation(g1[:, t, :], gy[t].indirect(entries(lists["n1"], c * HALF, HALF)), COPY)
                nc.scalar.activation(g2[:, t, :], gy[t].indirect(entries(lists["n2"], c * HALF, HALF)), COPY, scale=0.75)
            z_bf = sb("z_bf%d" % c, [P, HALF, PACK], BF16, tag=("w2_raw", "zq0_codes")[c])
            nc.vector.tensor_tensor(z_bf[:].rearrange("p (c i) t -> p c t i", i=4),
                                    g1.rearrange("p t (c i) -> p c t i", i=4),
                                    g2.rearrange("p t (c i) -> p c t i", i=4), ADD)
            return quantised("zq%d" % c, z_bf[:].rearrange("p s t -> p (s t)"), HALF)

        def h_half(c, z_q):
            for t in range(PACK):
                product(h_bank[t][:, halves[c]], w2_q, t, z_q[0][:], z_q[1][:])
                nc.vector.tensor_copy(h_win[t][:, halves[c]], h_bank[t][:, halves[c]])

        z_q = z_half(0, sb("g1_0", [P, PACK, HALF], F32)[:], sb("g2_0", [P, PACK, HALF], F32)[:])
        h_win = [sb("h_win%d" % t, [P, 2 * S], F32, tag=tag) for t, tag in enumerate(("g1_0", "g2_0", None))] + [h_last]
        h_half(0, z_q)
        for t in range(1, last):
            nc.vector.tensor_scalar(ys[t], y[t][:], 0.75, None, MULT)
        g_late = sb("g_late", [P, 2, PACK, HALF], F32, tag="gain")
        z_q = z_half(1, g_late[:, 0], g_late[:, 1])
        h_half(1, z_q)
        y_win.append(sb("y_win_last", [P, S], F32, tag="zq0_codes"))
        ys.append(y_win[last][:])
        nc.vector.tensor_scalar(ys[last], y[last][:], 0.75, None, MULT)

        out_rows = out.rearrange("(p t) s -> p t s", t=PACK)
        first = [sb("first%d" % t, [P, S], F32) for t in range(PACK)]
        second = [sb("second%d" % t, [P, S], F32) for t in range(PACK)]
        res = [sb("res%d" % t, [P, S], F32) for t in range(PACK)]

        def first_term(t, fetched, start, width):
            cols = slice(start, start + width)
            nc.scalar.activation(fetched[:, cols], y_win[t][:].indirect(entries(lists["n4"], start, width)), COPY)
            nc.vector.tensor_tensor(first[t][:, cols], h_bank[t][:, cols], fetched[:, cols], MULT)

        def second_term(t):
            h3 = sb("h3_%d" % t, [P, S], F32)
            nc.scalar.activation(h3[:], h_win[t][:].indirect(lists["n3"][:]), COPY)
            nc.vector.tensor_tensor(second[t][:], h3[:], ys[t], MULT)

        def finish(engine, t, start, width):
            cols = slice(start, start + width)
            engine.tensor_tensor(res[t][:, cols], first[t][:, cols], second[t][:, cols], SUB)
            nc.sync.dma_start(out_rows[:, t, cols], res[t][:, cols])

        for t in range(last):
            first_term(t, h_win[t][:, S:], 0, S)
        for t in range(last):
            second_term(t)
            finish(nc.vector, t, 0, S)
        second_term(last)
        y4_last = sb("y4_last", [P, S], F32, tag="g1_0")
        for start, width in ((0, HALF), (HALF, HALF // 2), (HALF + HALF // 2, HALF // 2)):
            first_term(last, y4_last[:], start, width)
            finish(nc.vector, last, start, width)
